import numpy as np
import ml_dtypes


def mxq(x, axis, fmt="e4m3"):
    dtype, down = {"e4m3": (ml_dtypes.float8_e4m3fn, 7), "e5m2": (ml_dtypes.float8_e5m2, 14)}[fmt]
    v = np.moveaxis(np.asarray(x, np.float32).astype(ml_dtypes.bfloat16).astype(np.float64), axis, -1)
    blocks = v.reshape(v.shape[:-1] + (-1, 32))
    amax = np.abs(blocks).max(-1, keepdims=True)
    byte = np.maximum(np.where(amax > 0, np.frexp(amax)[1] - 1 + 127, 0) - down, 1)
    scale = np.exp2(byte - 127.0)
    codes = (blocks / scale).astype(np.float32).astype(dtype).astype(np.float64)
    return np.moveaxis((codes * scale).reshape(v.shape), -1, axis)


WIDE = False


def mx_kscale(k):
    if not WIDE:
        return np.ones(k)
    levels = np.array([10, -10, 5, -5, 0])
    if k % 512:
        return np.exp2(np.random.permutation(np.resize(levels, k // 32))).repeat(32)
    a = np.empty((k // 512, 16))
    for p in range(k // 512):
        a[p, :8] = np.random.permutation(np.resize(levels, 8))
        for g in range(8):
            far = levels[np.abs(levels - a[p, g]) >= 10]
            a[p, g + 8] = far[np.random.randint(len(far))]
    return np.exp2(a.ravel()).repeat(32)


def f64(x):
    return np.asarray(x).astype(np.float64)


def striped(idx):
    return np.tile(idx.reshape(-1, 16).T, (8, 1)).astype(np.uint16)


def unstriped(offs):
    return offs[:16].T.reshape(-1).astype(np.int64)


E2M1 = np.array([0.0, 0.5, 1.0, 1.5, 2.0, 3.0, 4.0, 6.0, -0.0, -0.5, -1.0, -1.5, -2.0, -3.0, -4.0, -6.0])


def pack_weight(w, fmt):
    k, n = w.shape
    w = f64(np.asarray(w, np.float32).astype(ml_dtypes.bfloat16)).reshape(k // 32, 32, n)
    amax = np.abs(w).max(1)
    if fmt == "e4m3":
        byte = np.frexp(amax)[1] - 1 + 127 - 7
    else:
        mant, ex = np.frexp(amax / 6.0)
        byte = np.where(mant > 0.5, ex, ex - 1) + 127
    byte = np.clip(np.where(amax > 0, byte, 1), 1, 254)
    scaled = (w * np.exp2(127.0 - byte)[:, None, :]).reshape(k, n).astype(np.float32)
    by_word = np.ascontiguousarray(scaled.reshape(k // 512, 128, 4, n).transpose(0, 1, 3, 2))
    if fmt == "e4m3":
        words = by_word.astype(ml_dtypes.float8_e4m3fn).view(np.uint8)
    else:
        c = by_word.astype(ml_dtypes.float4_e2m1fn).view(np.uint8) & 0xF
        words = (c[..., 0::2] | (c[..., 1::2] << 4)).reshape(k // 512, 128, 2 * n)
    return np.ascontiguousarray(words), np.ascontiguousarray(byte.astype(np.uint8).reshape(k // 512, 16, n))


def unpack_weight(words, scales, fmt):
    g, _, n = scales.shape
    words = np.ascontiguousarray(words).reshape(g, 128, n, -1)
    if fmt == "e4m3":
        vals = words.view(ml_dtypes.float8_e4m3fn).astype(np.float64)
    else:
        nib = np.empty((g, 128, n, 4), np.uint8)
        nib[..., 0::2] = words & 0xF
        nib[..., 1::2] = words >> 4
        vals = E2M1[nib]
    vals = vals * np.repeat(np.exp2(scales.astype(np.float64) - 127.0), 8, axis=1)[..., None]
    return vals.transpose(0, 1, 3, 2).reshape(g * 512, n)


def gelu(v):
    return 0.5 * v * (1.0 + np.tanh(np.sqrt(2.0 / np.pi) * (v + 0.044715 * v**3)))


def bf(x):
    return np.asarray(x, np.float32).astype(ml_dtypes.bfloat16)


def planes(Y):
    n, m = Y.shape
    b = f64(bf(Y)).reshape(n // 32, 32, m)
    amax = np.abs(b).max(1)
    byte = np.clip(np.where(amax > 0, np.frexp(amax)[1] - 1 + 127 - 7, 1), 1, 254)
    codes = (b * np.exp2(127.0 - byte)[:, None, :]).reshape(n, m).astype(np.float32).astype(ml_dtypes.float8_e4m3fn).view(np.uint8)
    words = codes.reshape(n // 512, 128, 4, m).transpose(0, 1, 3, 2)
    return np.ascontiguousarray(words), np.ascontiguousarray(byte.astype(np.uint8).reshape(n // 512, 16, m))


K, H, N, T, S, T2, P = 1024, 512, 1024, 4096, 1024, 2048, 1024

def setup_inputs():
    n = np.random.standard_normal
    s = mx_kscale(K)[:, None]
    u = mx_kscale(H)[:, None]
    r = np.exp(0.8 * n(N))
    tab_words, tab_scales = pack_weight(n((K, T)) * s, "e4m3")
    w2_words, w2_scales = pack_weight(n((K, H)) / np.sqrt(K) / s * u.T, "e2m1")
    w3_words, w3_scales = pack_weight(1.2 * n((H, N)) / np.sqrt(H) / u, "e2m1")
    return {
        "tab_words": tab_words, "tab_scales": tab_scales,
        "offs": striped(np.random.permutation(T)[:S]),
        "offs2": striped(np.random.permutation(T2)[:S]),
        "offs3": striped(np.random.permutation(T2)[:P]),
        "page0": (n((H, T2)) * u).astype(np.float32),
        "w1": (n((K, H)) / np.sqrt(K) / s * u.T).astype(np.float32),
        "w2_words": w2_words, "w2_scales": w2_scales,
        "w3_words": w3_words, "w3_scales": w3_scales,
        "w4": (0.7 * n((H, N)) / np.sqrt(H) / u * r).astype(np.float32),
        "gain": (r * np.exp(0.3 * n(N))).astype(np.float32),
    }

def reference(tab_words, tab_scales, offs, offs2, offs3, page0, w1, w2_words, w2_scales, w3_words, w3_scales, w4, gain):
    v = unpack_weight(tab_words, tab_scales, "e4m3")[:, unstriped(offs)]
    cap = mxq(f64(w1), 0, "e4m3").T @ v
    base = unpack_weight(w2_words, w2_scales, "e2m1").T @ v
    page = f64(page0).copy()
    l2 = unstriped(offs2)
    old = page[:, l2]
    page[:, l2] = np.minimum(old, cap) + np.maximum(old, base)
    x = page[:, unstriped(offs3)]
    xq = mxq(x, 0, "e4m3")
    e = unpack_weight(w3_words, w3_scales, "e2m1").T @ xq
    d = mxq(f64(w4), 0, "e4m3").T @ xq
    y = f64(gain)[:, None] * np.tanh(e) + d
    words, scales = planes(y)
    return y, words, scales

@@ -1,0 +1,307 @@
+from contextlib import ExitStack
+
+import concourse.mybir as mybir
+
+K, H, N, T, S, T2, M = 1024, 512, 1024, 4096, 1024, 2048, 1024
+FLOPS = 2 * (2 * K * H * S) + 2 * (2 * H * N * M)
+
+F32 = mybir.dt.float32
+BF16 = mybir.dt.bfloat16
+I32 = mybir.dt.int32
+U32 = mybir.dt.uint32
+U16 = mybir.dt.uint16
+U8 = mybir.dt.uint8
+FP8X4 = mybir.dt.float8_e4m3fn_x4
+FP4X4 = mybir.dt.float4_e2m1fn_x4
+ALU = mybir.AluOpType
+ACT = mybir.ActivationFunctionType
+
+P = 128
+PACK = 4
+PASS = P * PACK
+BANK = 512
+CHUNK = 256
+CHUNKS = M // CHUNK
+PER_COL = 16
+
+
+def interleave(copy, dst, src):
+    copy(dst.rearrange("p (c i t) -> p c t i", i=4, t=PACK), src.rearrange("p (t c i) -> p c t i", i=4, t=PACK))
+
+
+def tile_list_applicant_profile_update_kernel(
+    tc, tab_words, tab_scales, offs, offs2, offs3, page0, w1, w2_words, w2_scales, w3_words, w3_scales, w4, gain,
+    out_0, out_1, out_2,
+):
+    nc = tc.nc
+    with ExitStack() as ctx:
+        keep = ctx.enter_context(tc.tile_pool(name="keep", bufs=1))
+        ring = ctx.enter_context(tc.tile_pool(name="ring", bufs=2))
+        psum = ctx.enter_context(tc.psum_pool(name="psum", bufs=4))
+
+        def held(name, shape, dtype):
+            return keep.tile(shape, dtype, name=name, align_bytes=64)
+
+        list1 = held("list1", [P, S // PER_COL], U16)
+        list2 = held("list2", [P, S // PER_COL], U16)
+        list3 = held("list3", [P, M // PER_COL], U16)
+        page = [held("page%d" % t, [P, T2], F32) for t in range(PACK)]
+        tab_w = [held("tab_w%d" % a, [P, T], U32) for a in range(2)]
+        tab_s = held("tab_s", [P, T], U8)
+        v_w = [held("v_w%d" % a, [P, S], U32) for a in range(2)]
+        v_s = [held("v_s%d" % a, [P, S], U8) for a in range(2)]
+        w2_raw = held("w2_raw", [P, 2 * 2 * PASS], U8)
+        w3_raw = held("w3_raw", [P, 2 * 2 * PASS], U8)
+        w2s_raw = held("w2s_raw", [P, 2 * PASS], U8)
+        w3s_raw = held("w3s_raw", [P, 2 * PASS], U8)
+        w2_w = held("w2_w", [P, 2 * 2 * PASS], U8)
+        w3_w = held("w3_w", [P, 2 * 2 * PASS], U8)
+        w2_s = held("w2_s", [P, 2 * PASS], U8)
+        w3_s = held("w3_s", [P, 2 * PASS], U8)
+        w1_w = [held("w1_w%d" % a, [P, PASS], U32) for a in range(2)]
+        w1_s = [held("w1_s%d" % a, [P, PASS], U8) for a in range(2)]
+        w4_w = [held("w4_w%d" % g, [P, PASS], U32) for g in range(2)]
+        w4_s = [held("w4_s%d" % g, [P, PASS], U8) for g in range(2)]
+        gains = held("gains", [P, 2, PACK], F32)
+        parts = [held("parts%d" % t, [P, 2 * S], F32) for t in range(PACK)]
+        spare = [held("spare%d" % i, [P, PACK * CHUNK], F32) for i in range(2)]
+        y_w = held("y_w", [P, 2 * M], U32)
+        y_s = held("y_s", [P, 2 * M], U8)
+
+        page_rows = page0.rearrange("(p t) c -> t p c", t=PACK)
+
+        def load_page(t):
+            nc.sync.dma_start(out=page[t][:], in_=page_rows[t])
+
+        def load_tab(a):
+            nc.sync.dma_start(out=tab_w[a][:].bitcast(I32), in_=tab_words[a].rearrange("p c i -> p (c i)").bitcast(I32))
+
+        def load_float_weight(rows):
+            raw = ring.tile([P, PACK, PASS], F32, name="w_raw", bufs=3)
+            nc.sync.dma_start(out=raw[:], in_=rows.rearrange("(p j) c -> p j c", j=PACK))
+            return raw
+
+        def quantize_weight(raw, words, scales):
+            dealt = ring.tile([P, PACK * PASS], BF16, name="w_dealt", align_bytes=64)
+            nc.scalar.copy(
+                dealt[:].rearrange("p (t m j) -> p m j t", t=PACK, j=PACK),
+                raw[:].rearrange("p j (m t) -> p m j t", t=PACK),
+            )
+            nc.vector.quantize_mx(out=words[:].bitcast(FP8X4), scales=scales[:], in_=dealt[:])
+
+        def deal(dst, src):
+            nc.vector.tensor_copy(
+                dst.rearrange("p (a t m) -> p a m t", a=2, t=PACK),
+                src.rearrange("p (a m t) -> p a m t", a=2, t=PACK),
+            )
+
+        nc.vector.memset(tab_s[:].bitcast(I32), 0)
+        nc.vector.memset(v_s[1][:].bitcast(I32), 0)
+        nc.vector.memset(w3s_raw[:].bitcast(I32), 0)
+        nc.vector.memset(w2s_raw[:].bitcast(I32), 0)
+        nc.sync.dma_start(list2[:], offs2)
+        load_page(0)
+        for q in range(4):
+            nc.sync.dma_start(
+                out=tab_s[32 * q : 32 * q + 8, :].bitcast(I32),
+                in_=tab_scales.bitcast(I32)[:, 4 * q : 4 * q + 4, :],
+            )
+        nc.sync.dma_start(list1[:], offs)
+        load_tab(0)
+        nc.sync.dma_start(
+            out=w2_raw[:].bitcast(I32).rearrange("p (a c) -> p a c", a=2),
+            in_=w2_words.bitcast(I32).rearrange("a p c -> p a c"),
+        )
+        load_page(1)
+        for q in range(4):
+            nc.sync.dma_start(
+                out=w2s_raw[32 * q : 32 * q + 4, :].bitcast(I32).rearrange("r (a c) -> r a c", a=2),
+                in_=w2_scales.bitcast(I32)[:, 4 * q : 4 * q + 4, :].rearrange("a r c -> r a c"),
+            )
+        load_page(2)
+        load_tab(1)
+        w1_raw = [load_float_weight(w1[a * PASS : (a + 1) * PASS, :]) for a in range(2)]
+        load_page(3)
+        nc.sync.dma_start(list3[:], offs3)
+        w4_raw = [load_float_weight(w4[:, g * PASS : (g + 1) * PASS]) for g in range(2)]
+        nc.sync.dma_start(out=w3_raw[:].bitcast(I32), in_=w3_words.bitcast(I32)[0])
+        for q in range(4):
+            nc.sync.dma_start(
+                out=w3s_raw[32 * q : 32 * q + 4, :].bitcast(I32),
+                in_=w3_scales.bitcast(I32)[0, 4 * q : 4 * q + 4, :],
+            )
+        nc.sync.dma_start(out=gains[:], in_=gain.rearrange("(g p t) -> p g t", g=2, t=PACK))
+
+        def fetch_old(t):
+            nc.vector.tensor_copy(parts[t][:, 0:S], page[t][:].indirect(list2[:]))
+
+        def fetch_x(t, c, dst):
+            cols = slice(c * CHUNK // PER_COL, (c + 1) * CHUNK // PER_COL)
+            nc.vector.tensor_copy(dst[:, t * CHUNK : (t + 1) * CHUNK], page[t][:].indirect(list3[:, cols]))
+
+        fetch_old(0)
+        nc.vector.tensor_copy(v_s[0][:], tab_s[:].indirect(list1[:]))
+        nc.scalar.dma_start(out=v_s[1][0:100, :].bitcast(I32), in_=v_s[0][4:104, :].bitcast(I32))
+        nc.vector.tensor_copy(v_w[0][:], tab_w[0][:].indirect(list1[:]))
+        fetch_old(1)
+        fetch_old(2)
+        deal(w2_w[:].bitcast(U16), w2_raw[:].bitcast(U16))
+        deal(w2_s[:], w2s_raw[:])
+        for h in range(S // BANK):
+            nc.vector.tensor_copy(
+                v_w[1][:, h * BANK : (h + 1) * BANK],
+                tab_w[1][:].indirect(list1[:, h * BANK // PER_COL : (h + 1) * BANK // PER_COL]),
+            )
+
+        def larger(t):
+            for h in range(S // BANK):
+                cols = slice(h * BANK, (h + 1) * BANK)
+                base = psum.tile([P, BANK], F32, name="bank_a")
+                for a in range(2):
+                    at = a * PACK + t
+                    nc.tensor.matmul_mx(
+                        out=base[:],
+                        lhsT=w2_w[:, 2 * P * at : 2 * P * (at + 1)].bitcast(FP4X4),
+                        lhsT_scale=w2_s[:, P * at : P * (at + 1)],
+                        rhs=v_w[a][:, cols].bitcast(FP8X4),
+                        rhs_scale=v_s[a][:, cols],
+                        start=(a == 0),
+                        stop=(a == 1),
+                    )
+                nc.vector.tensor_tensor(
+                    parts[t][:, S + h * BANK : S + (h + 1) * BANK], parts[t][:, cols], base[:], ALU.max
+                )
+
+        def smaller(t):
+            for h in range(S // BANK):
+                cols = slice(h * BANK, (h + 1) * BANK)
+                cap = psum.tile([P, BANK], F32, name="bank_b")
+                for a in range(2):
+                    nc.tensor.matmul_mx(
+                        out=cap[:],
+                        lhsT=w1_w[a][:, P * t : P * (t + 1)].bitcast(FP8X4),
+                        lhsT_scale=w1_s[a][:, P * t : P * (t + 1)],
+                        rhs=v_w[a][:, cols].bitcast(FP8X4),
+                        rhs_scale=v_s[a][:, cols],
+                        start=(a == 0),
+                        stop=(a == 1),
+                    )
+                nc.vector.tensor_tensor(parts[t][:, cols], parts[t][:, cols], cap[:], ALU.min)
+
+        def put(t):
+            nc.vector.tensor_tensor(page[t][:].indirect(list2[:]), parts[t][:, 0:S], parts[t][:, S : 2 * S], ALU.add)
+
+        for t in range(PACK - 1):
+            larger(t)
+        quantize_weight(w1_raw[0], w1_w[0], w1_s[0])
+        fetch_old(PACK - 1)
+        quantize_weight(w1_raw[1], w1_w[1], w1_s[1])
+        larger(PACK - 1)
+        smaller(0)
+        for t in range(PACK):
+            if t + 1 < PACK:
+                smaller(t + 1)
+            put(t)
+            if t == 0:
+                for g in range(2):
+                    quantize_weight(w4_raw[g], w4_w[g], w4_s[g])
+                deal(w3_w[:].bitcast(U16), w3_raw[:].bitcast(U16))
+                deal(w3_s[:], w3s_raw[:])
+            fetch_x(t, 0, spare[0])
+
+        last = parts[PACK - 1]
+        x_f32 = [spare[0][:], last[:, 0 : PACK * CHUNK], spare[0][:], spare[1][:]]
+
+        def quantize_x(c):
+            if c == 0:
+                x_bf = last[:, 2 * CHUNK : PACK * CHUNK].bitcast(BF16)
+            else:
+                x_tile = ring.tile([P, PACK * CHUNK], BF16, name="x_bf", align_bytes=64)
+                x_bf = x_tile[:]
+            interleave(nc.scalar.copy, x_bf, x_f32[c])
+            x_w = ring.tile([P, CHUNK], U32, name="x_w", align_bytes=64)
+            x_s = ring.tile([P, CHUNK], U8, name="x_s", align_bytes=64)
+            return x_bf, x_w, x_s
+
+        def features(c, g, x_w, x_s):
+            if g == 1:
+                th = spare[c % 2][:]
+            else:
+                th_tile = ring.tile([P, PACK * CHUNK], F32, name="th")
+                th = th_tile[:]
+            y = ring.tile([P, PACK * CHUNK], F32, name="y", bufs=4)
+            for u in range(2):
+                e = psum.tile([P, BANK], F32, name="bank_a")
+                d = psum.tile([P, BANK], F32, name="bank_b")
+                for i in range(2):
+                    gt = g * PACK + 2 * u + i
+                    nc.tensor.matmul_mx(
+                        out=e[:, i * CHUNK : (i + 1) * CHUNK],
+                        lhsT=w3_w[:, 2 * P * gt : 2 * P * (gt + 1)].bitcast(FP4X4),
+                        lhsT_scale=w3_s[:, P * gt : P * (gt + 1)],
+                        rhs=x_w[:].bitcast(FP8X4),
+                        rhs_scale=x_s[:],
+                        start=True,
+                        stop=True,
+                    )
+                for i in range(2):
+                    t = 2 * u + i
+                    nc.tensor.matmul_mx(
+                        out=d[:, i * CHUNK : (i + 1) * CHUNK],
+                        lhsT=w4_w[g][:, P * t : P * (t + 1)].bitcast(FP8X4),
+                        lhsT_scale=w4_s[g][:, P * t : P * (t + 1)],
+                        rhs=x_w[:].bitcast(FP8X4),
+                        rhs_scale=x_s[:],
+                        start=True,
+                        stop=True,
+                    )
+                nc.scalar.activation(th[:, u * BANK : (u + 1) * BANK], e[:], ACT.Tanh)
+                for i in range(2):
+                    t = 2 * u + i
+                    nc.vector.scalar_tensor_tensor(
+                        y[:, t * CHUNK : (t + 1) * CHUNK],
+                        th[:, t * CHUNK : (t + 1) * CHUNK],
+                        gains[:, g, t : t + 1],
+                        d[:, i * CHUNK : (i + 1) * CHUNK],
+                        ALU.mult,
+                        ALU.add,
+                    )
+            cols = slice(c * CHUNK, (c + 1) * CHUNK)
+            nc.sync.dma_start(
+                out=out_0[g * PASS : (g + 1) * PASS, cols].rearrange("(p t) m -> p t m", t=PACK),
+                in_=y[:].rearrange("p (t m) -> p t m", t=PACK),
+            )
+            return y
+
+        def planes(c, g, y):
+            y_bf = ring.tile([P, PACK * CHUNK], BF16, name="y_bf", bufs=3, align_bytes=64)
+            on_vector = c == 2 or (c, g) == (3, 1)
+            interleave(nc.vector.tensor_copy if on_vector else nc.scalar.copy, y_bf[:], y[:])
+            at = slice(g * M + c * CHUNK, g * M + (c + 1) * CHUNK)
+            nc.vector.quantize_mx(out=y_w[:, at].bitcast(FP8X4), scales=y_s[:, at], in_=y_bf[:])
+            nc.sync.dma_start(
+                out=out_1[g].rearrange("p m t -> p (m t)").bitcast(I32)[:, c * CHUNK : (c + 1) * CHUNK],
+                in_=y_w[:, at].bitcast(I32),
+            )
+
+        x_bf, x_w, x_s = quantize_x(0)
+        for t in (0, 1):
+            fetch_x(t, 1, x_f32[1])
+        nc.vector.quantize_mx(out=x_w[:].bitcast(FP8X4), scales=x_s[:], in_=x_bf)
+        for t in (2, 3):
+            fetch_x(t, 1, x_f32[1])
+        for c in range(CHUNKS):
+            ys = [features(c, g, x_w, x_s) for g in range(2)]
+            if c + 1 < CHUNKS:
+                x_bf, x_w, x_s = quantize_x(c + 1)
+                nc.vector.quantize_mx(out=x_w[:].bitcast(FP8X4), scales=x_s[:], in_=x_bf)
+            if c + 2 < CHUNKS:
+                for t in range(PACK):
+                    fetch_x(t, c + 2, x_f32[c + 2])
+            for g in range(2):
+                planes(c, g, ys[g])
+        for q in range(4):
+            nc.sync.dma_start(
+                out=out_2.bitcast(I32)[:, 4 * q : 4 * q + 4, :].rearrange("g r m -> r g m"),
+                in_=y_s[32 * q : 32 * q + 4, :].bitcast(I32).rearrange("r (g m) -> r g m", g=2),
+            )

@@ -20,8 +20,10 @@ P = 128
 PACK = 4
 PASS = P * PACK
 BANK = 512
-CHUNK = 256
-CHUNKS = M // CHUNK
+WIDTHS = (128, 256, 256, 256, 128)
+STARTS = [sum(WIDTHS[:c]) for c in range(len(WIDTHS))]
+WIDEST = max(WIDTHS)
+SHIFT_ROWS = 112
 PER_COL = 16
 
 
@@ -53,18 +55,18 @@ def tile_list_applicant_profile_update_kernel(
         w2_raw = held("w2_raw", [P, 2 * 2 * PASS], U8)
         w3_raw = held("w3_raw", [P, 2 * 2 * PASS], U8)
         w2s_raw = held("w2s_raw", [P, 2 * PASS], U8)
-        w3s_raw = held("w3s_raw", [P, 2 * PASS], U8)
+        w3s_raw = held("w3s_raw", [P, PASS], U8)
         w2_w = held("w2_w", [P, 2 * 2 * PASS], U8)
         w3_w = held("w3_w", [P, 2 * 2 * PASS], U8)
         w2_s = held("w2_s", [P, 2 * PASS], U8)
-        w3_s = held("w3_s", [P, 2 * PASS], U8)
+        w3_s = [held("w3_s%d" % g, [P, PASS], U8) for g in range(2)]
         w1_w = [held("w1_w%d" % a, [P, PASS], U32) for a in range(2)]
         w1_s = [held("w1_s%d" % a, [P, PASS], U8) for a in range(2)]
         w4_w = [held("w4_w%d" % g, [P, PASS], U32) for g in range(2)]
         w4_s = [held("w4_s%d" % g, [P, PASS], U8) for g in range(2)]
         gains = held("gains", [P, 2, PACK], F32)
         parts = [held("parts%d" % t, [P, 2 * S], F32) for t in range(PACK)]
-        spare = [held("spare%d" % i, [P, PACK * CHUNK], F32) for i in range(2)]
+        spare = [held("spare%d" % i, [P, PACK * WIDEST], F32) for i in range(2)]
         y_w = held("y_w", [P, 2 * M], U32)
         y_s = held("y_s", [P, 2 * M], U8)
 
@@ -84,20 +86,24 @@ def tile_list_applicant_profile_update_kernel(
         def quantize_weight(raw, words, scales):
             dealt = ring.tile([P, PACK * PASS], BF16, name="w_dealt", align_bytes=64)
             nc.scalar.copy(
-                dealt[:].rearrange("p (t m j) -> p m j t", t=PACK, j=PACK),
-                raw[:].rearrange("p j (m t) -> p m j t", t=PACK),
+                dealt[:].rearrange("p (t m j) -> p m t j", t=PACK, j=PACK),
+                raw[:].rearrange("p j (m t) -> p m t j", t=PACK),
             )
             nc.vector.quantize_mx(out=words[:].bitcast(FP8X4), scales=scales[:], in_=dealt[:])
 
         def deal(dst, src):
             nc.vector.tensor_copy(
-                dst.rearrange("p (a t m) -> p a m t", a=2, t=PACK),
-                src.rearrange("p (a m t) -> p a m t", a=2, t=PACK),
+                dst.rearrange("p (a t m) -> p a m t", t=PACK, m=P),
+                src.rearrange("p (a m t) -> p a m t", t=PACK, m=P),
             )
+
+        def shift_up(queue, dst, src):
+            queue.dma_start(out=dst[0:SHIFT_ROWS, :].bitcast(I32), in_=src[4 : 4 + SHIFT_ROWS, :].bitcast(I32))
 
         nc.vector.memset(tab_s[:].bitcast(I32), 0)
         nc.vector.memset(v_s[1][:].bitcast(I32), 0)
         nc.vector.memset(w3s_raw[:].bitcast(I32), 0)
+        nc.vector.memset(w3_s[1][:].bitcast(I32), 0)
         nc.vector.memset(w2s_raw[:].bitcast(I32), 0)
         nc.sync.dma_start(list2[:], offs2)
         load_page(0)
@@ -127,21 +133,28 @@ def tile_list_applicant_profile_update_kernel(
         nc.sync.dma_start(out=w3_raw[:].bitcast(I32), in_=w3_words.bitcast(I32)[0])
         for q in range(4):
             nc.sync.dma_start(
-                out=w3s_raw[32 * q : 32 * q + 4, :].bitcast(I32),
-                in_=w3_scales.bitcast(I32)[0, 4 * q : 4 * q + 4, :],
+                out=w3s_raw[32 * q : 32 * q + 8, :].bitcast(I32),
+                in_=w3_scales.bitcast(I32)[0, 4 * q : 4 * q + 4, :].rearrange("r (g c) -> g r c", g=2),
             )
         nc.sync.dma_start(out=gains[:], in_=gain.rearrange("(g p t) -> p g t", g=2, t=PACK))
 
         def fetch_old(t):
             nc.vector.tensor_copy(parts[t][:, 0:S], page[t][:].indirect(list2[:]))
 
-        def fetch_x(t, c, dst):
-            cols = slice(c * CHUNK // PER_COL, (c + 1) * CHUNK // PER_COL)
-            nc.vector.tensor_copy(dst[:, t * CHUNK : (t + 1) * CHUNK], page[t][:].indirect(list3[:, cols]))
+        last = parts[PACK - 1]
+        x_rows = [spare[0][:, 0 : 2 * WIDTHS[0]].bitcast(BF16), last[:, 0 : 2 * WIDTHS[1]].bitcast(BF16)]
+        for c in range(2, len(WIDTHS)):
+            end = PACK * WIDTHS[c - 2]
+            x_rows.append(spare[c % 2][:, end - 2 * WIDTHS[c] : end].bitcast(BF16))
+
+        def fetch_x(t, c):
+            w = WIDTHS[c]
+            cols = slice(STARTS[c] // PER_COL, (STARTS[c] + w) // PER_COL)
+            nc.vector.tensor_copy(x_rows[c][:, t * w : (t + 1) * w], page[t][:].indirect(list3[:, cols]))
 
         fetch_old(0)
         nc.vector.tensor_copy(v_s[0][:], tab_s[:].indirect(list1[:]))
-        nc.scalar.dma_start(out=v_s[1][0:100, :].bitcast(I32), in_=v_s[0][4:104, :].bitcast(I32))
+        shift_up(nc.scalar, v_s[1], v_s[0])
         nc.vector.tensor_copy(v_w[0][:], tab_w[0][:].indirect(list1[:]))
         fetch_old(1)
         fetch_old(2)
@@ -206,48 +219,54 @@ def tile_list_applicant_profile_update_kernel(
                 for g in range(2):
                     quantize_weight(w4_raw[g], w4_w[g], w4_s[g])
                 deal(w3_w[:].bitcast(U16), w3_raw[:].bitcast(U16))
-                deal(w3_s[:], w3s_raw[:])
-            fetch_x(t, 0, spare[0])
+                deal(w3_s[0][:], w3s_raw[:])
+                shift_up(nc.sync, w3_s[1], w3_s[0])
+            fetch_x(t, 0)
 
-        last = parts[PACK - 1]
-        x_f32 = [spare[0][:], last[:, 0 : PACK * CHUNK], spare[0][:], spare[1][:]]
-
-        def quantize_x(c):
+        def interleave_x(c):
+            w = WIDTHS[c]
             if c == 0:
-                x_bf = last[:, 2 * CHUNK : PACK * CHUNK].bitcast(BF16)
+                x_bf = x_rows[1][:, 2 * WIDTHS[1] : PACK * WIDTHS[1]]
             else:
-                x_tile = ring.tile([P, PACK * CHUNK], BF16, name="x_bf", align_bytes=64)
+                x_tile = ring.tile([P, PACK * w], BF16, name="x_bf", align_bytes=64)
                 x_bf = x_tile[:]
-            interleave(nc.scalar.copy, x_bf, x_f32[c])
-            x_w = ring.tile([P, CHUNK], U32, name="x_w", align_bytes=64)
-            x_s = ring.tile([P, CHUNK], U8, name="x_s", align_bytes=64)
-            return x_bf, x_w, x_s
+            interleave(nc.scalar.copy, x_bf, x_rows[c])
+            return x_bf
+
+        def quantize_x(c, x_bf):
+            x_w = ring.tile([P, WIDTHS[c]], U32, name="x_w", align_bytes=64)
+            x_s = ring.tile([P, WIDTHS[c]], U8, name="x_s", align_bytes=64)
+            nc.vector.quantize_mx(out=x_w[:].bitcast(FP8X4), scales=x_s[:], in_=x_bf)
+            return x_w, x_s
 
         def features(c, g, x_w, x_s):
+            w = WIDTHS[c]
+            per_bank = BANK // w
             if g == 1:
-                th = spare[c % 2][:]
+                th = spare[c % 2][:, 0 : PACK * w]
             else:
-                th_tile = ring.tile([P, PACK * CHUNK], F32, name="th")
+                th_tile = ring.tile([P, PACK * w], F32, name="th")
                 th = th_tile[:]
-            y = ring.tile([P, PACK * CHUNK], F32, name="y", bufs=4)
-            for u in range(2):
+            y = ring.tile([P, PACK * w], F32, name="y", bufs=4)
+            for t0 in range(0, PACK, per_bank):
                 e = psum.tile([P, BANK], F32, name="bank_a")
                 d = psum.tile([P, BANK], F32, name="bank_b")
-                for i in range(2):
-                    gt = g * PACK + 2 * u + i
+                for i in range(per_bank):
+                    t = t0 + i
+                    gt = g * PACK + t
                     nc.tensor.matmul_mx(
-                        out=e[:, i * CHUNK : (i + 1) * CHUNK],
+                        out=e[:, i * w : (i + 1) * w],
                         lhsT=w3_w[:, 2 * P * gt : 2 * P * (gt + 1)].bitcast(FP4X4),
-                        lhsT_scale=w3_s[:, P * gt : P * (gt + 1)],
+                        lhsT_scale=w3_s[g][:, P * t : P * (t + 1)],
                         rhs=x_w[:].bitcast(FP8X4),
                         rhs_scale=x_s[:],
                         start=True,
                         stop=True,
                     )
-                for i in range(2):
-                    t = 2 * u + i
+                for i in range(per_bank):
+                    t = t0 + i
                     nc.tensor.matmul_mx(
-                        out=d[:, i * CHUNK : (i + 1) * CHUNK],
+                        out=d[:, i * w : (i + 1) * w],
                         lhsT=w4_w[g][:, P * t : P * (t + 1)].bitcast(FP8X4),
                         lhsT_scale=w4_s[g][:, P * t : P * (t + 1)],
                         rhs=x_w[:].bitcast(FP8X4),
@@ -255,49 +274,48 @@ def tile_list_applicant_profile_update_kernel(
                         start=True,
                         stop=True,
                     )
-                nc.scalar.activation(th[:, u * BANK : (u + 1) * BANK], e[:], ACT.Tanh)
-                for i in range(2):
-                    t = 2 * u + i
+                nc.scalar.activation(th[:, t0 * w : t0 * w + BANK], e[:], ACT.Tanh)
+                for i in range(per_bank):
+                    t = t0 + i
                     nc.vector.scalar_tensor_tensor(
-                        y[:, t * CHUNK : (t + 1) * CHUNK],
-                        th[:, t * CHUNK : (t + 1) * CHUNK],
+                        y[:, t * w : (t + 1) * w],
+                        th[:, t * w : (t + 1) * w],
                         gains[:, g, t : t + 1],
-                        d[:, i * CHUNK : (i + 1) * CHUNK],
+                        d[:, i * w : (i + 1) * w],
                         ALU.mult,
                         ALU.add,
                     )
-            cols = slice(c * CHUNK, (c + 1) * CHUNK)
             nc.sync.dma_start(
-                out=out_0[g * PASS : (g + 1) * PASS, cols].rearrange("(p t) m -> p t m", t=PACK),
+                out=out_0[g * PASS : (g + 1) * PASS, STARTS[c] : STARTS[c] + w].rearrange("(p t) m -> p t m", t=PACK),
                 in_=y[:].rearrange("p (t m) -> p t m", t=PACK),
             )
             return y
 
         def planes(c, g, y):
-            y_bf = ring.tile([P, PACK * CHUNK], BF16, name="y_bf", bufs=3, align_bytes=64)
-            on_vector = c == 2 or (c, g) == (3, 1)
+            w = WIDTHS[c]
+            y_bf = ring.tile([P, PACK * w], BF16, name="y_bf", bufs=3, align_bytes=64)
+            on_vector = (c, g) in ((2, 1), (3, 0), (3, 1), (4, 1))
             interleave(nc.vector.tensor_copy if on_vector else nc.scalar.copy, y_bf[:], y[:])
-            at = slice(g * M + c * CHUNK, g * M + (c + 1) * CHUNK)
+            at = slice(g * M + STARTS[c], g * M + STARTS[c] + w)
             nc.vector.quantize_mx(out=y_w[:, at].bitcast(FP8X4), scales=y_s[:, at], in_=y_bf[:])
             nc.sync.dma_start(
-                out=out_1[g].rearrange("p m t -> p (m t)").bitcast(I32)[:, c * CHUNK : (c + 1) * CHUNK],
+                out=out_1[g].rearrange("p m t -> p (m t)").bitcast(I32)[:, STARTS[c] : STARTS[c] + w],
                 in_=y_w[:, at].bitcast(I32),
             )
 
-        x_bf, x_w, x_s = quantize_x(0)
+        x_bf = interleave_x(0)
         for t in (0, 1):
-            fetch_x(t, 1, x_f32[1])
-        nc.vector.quantize_mx(out=x_w[:].bitcast(FP8X4), scales=x_s[:], in_=x_bf)
+            fetch_x(t, 1)
+        x_w, x_s = quantize_x(0, x_bf)
         for t in (2, 3):
-            fetch_x(t, 1, x_f32[1])
-        for c in range(CHUNKS):
+            fetch_x(t, 1)
+        for c in range(len(WIDTHS)):
             ys = [features(c, g, x_w, x_s) for g in range(2)]
-            if c + 1 < CHUNKS:
-                x_bf, x_w, x_s = quantize_x(c + 1)
-                nc.vector.quantize_mx(out=x_w[:].bitcast(FP8X4), scales=x_s[:], in_=x_bf)
-            if c + 2 < CHUNKS:
+            if c + 1 < len(WIDTHS):
+                x_w, x_s = quantize_x(c + 1, interleave_x(c + 1))
+            if c + 2 < len(WIDTHS):
                 for t in range(PACK):
-                    fetch_x(t, c + 2, x_f32[c + 2])
+                    fetch_x(t, c + 2)
             for g in range(2):
                 planes(c, g, ys[g])
         for q in range(4):

@@ -20,9 +20,8 @@ P = 128
 PACK = 4
 PASS = P * PACK
 BANK = 512
-WIDTHS = (128, 256, 256, 256, 128)
+WIDTHS = (256, 512, 256)
 STARTS = [sum(WIDTHS[:c]) for c in range(len(WIDTHS))]
-WIDEST = max(WIDTHS)
 SHIFT_ROWS = 112
 PER_COL = 16
 
@@ -66,7 +65,6 @@ def tile_list_applicant_profile_update_kernel(
         w4_s = [held("w4_s%d" % g, [P, PASS], U8) for g in range(2)]
         gains = held("gains", [P, 2, PACK], F32)
         parts = [held("parts%d" % t, [P, 2 * S], F32) for t in range(PACK)]
-        spare = [held("spare%d" % i, [P, PACK * WIDEST], F32) for i in range(2)]
         y_w = held("y_w", [P, 2 * M], U32)
         y_s = held("y_s", [P, 2 * M], U8)
 
@@ -79,7 +77,7 @@ def tile_list_applicant_profile_update_kernel(
             nc.sync.dma_start(out=tab_w[a][:].bitcast(I32), in_=tab_words[a].rearrange("p c i -> p (c i)").bitcast(I32))
 
         def load_float_weight(rows):
-            raw = ring.tile([P, PACK, PASS], F32, name="w_raw", bufs=3)
+            raw = ring.tile([P, PACK, PASS], F32, name="w_raw", tag="staging", bufs=6)
             nc.sync.dma_start(out=raw[:], in_=rows.rearrange("(p j) c -> p j c", j=PACK))
             return raw
 
@@ -141,16 +139,24 @@ def tile_list_applicant_profile_update_kernel(
         def fetch_old(t):
             nc.vector.tensor_copy(parts[t][:, 0:S], page[t][:].indirect(list2[:]))
 
-        last = parts[PACK - 1]
-        x_rows = [spare[0][:, 0 : 2 * WIDTHS[0]].bitcast(BF16), last[:, 0 : 2 * WIDTHS[1]].bitcast(BF16)]
-        for c in range(2, len(WIDTHS)):
-            end = PACK * WIDTHS[c - 2]
-            x_rows.append(spare[c % 2][:, end - 2 * WIDTHS[c] : end].bitcast(BF16))
+        x_rows = held("x_rows", [P, 2 * M], BF16)
+        x_bf = [held("x_bf%d" % i, [P, PACK * WIDTHS[i]], BF16) for i in range(2)]
 
-        def fetch_x(t, c):
-            w = WIDTHS[c]
-            cols = slice(STARTS[c] // PER_COL, (STARTS[c] + w) // PER_COL)
-            nc.vector.tensor_copy(x_rows[c][:, t * w : (t + 1) * w], page[t][:].indirect(list3[:, cols]))
+        def x_slots(c):
+            return x_bf[c % 2][:].rearrange("p (m t) -> p m t", t=PACK)
+
+        def look_up_x(t, start, stop):
+            return page[t][:].indirect(list3[:, start // PER_COL : stop // PER_COL])
+
+        def fetch_x_row(t):
+            nc.vector.tensor_copy(x_rows[:, t * M : (t + 1) * M], look_up_x(t, 0, M))
+
+        def lay_x_rows(c):
+            rows = x_rows[:].rearrange("p (t m) -> p m t", t=2)
+            nc.scalar.copy(x_slots(c)[:, :, 0:2], rows[:, STARTS[c] : STARTS[c] + WIDTHS[c], :])
+
+        def fetch_x_slot(t, c):
+            nc.vector.tensor_copy(x_slots(c)[:, :, t], look_up_x(t, STARTS[c], STARTS[c] + WIDTHS[c]))
 
         fetch_old(0)
         nc.vector.tensor_copy(v_s[0][:], tab_s[:].indirect(list1[:]))
@@ -214,6 +220,14 @@ def tile_list_applicant_profile_update_kernel(
         for t in range(PACK):
             if t + 1 < PACK:
                 smaller(t + 1)
+            if t in (1, 2):
+                fetch_x_row(t - 1)
+            if t == 2:
+                for c in (0, 1):
+                    lay_x_rows(c)
+            if t == 3:
+                for c in (0, 1):
+                    fetch_x_slot(2, c)
             put(t)
             if t == 0:
                 for g in range(2):
@@ -221,33 +235,19 @@ def tile_list_applicant_profile_update_kernel(
                 deal(w3_w[:].bitcast(U16), w3_raw[:].bitcast(U16))
                 deal(w3_s[0][:], w3s_raw[:])
                 shift_up(nc.sync, w3_s[1], w3_s[0])
-            fetch_x(t, 0)
 
-        def interleave_x(c):
+        def quantize_x(c):
             w = WIDTHS[c]
-            if c == 0:
-                x_bf = x_rows[1][:, 2 * WIDTHS[1] : PACK * WIDTHS[1]]
-            else:
-                x_tile = ring.tile([P, PACK * w], BF16, name="x_bf", align_bytes=64)
-                x_bf = x_tile[:]
-            interleave(nc.scalar.copy, x_bf, x_rows[c])
-            return x_bf
-
-        def quantize_x(c, x_bf):
-            x_w = ring.tile([P, WIDTHS[c]], U32, name="x_w", align_bytes=64)
-            x_s = ring.tile([P, WIDTHS[c]], U8, name="x_s", align_bytes=64)
-            nc.vector.quantize_mx(out=x_w[:].bitcast(FP8X4), scales=x_s[:], in_=x_bf)
+            x_w = ring.tile([P, w], U32, name="x_w", align_bytes=64)
+            x_s = ring.tile([P, w], U8, name="x_s", align_bytes=64)
+            nc.vector.quantize_mx(out=x_w[:].bitcast(FP8X4), scales=x_s[:], in_=x_bf[c % 2][:])
             return x_w, x_s
 
         def features(c, g, x_w, x_s):
             w = WIDTHS[c]
             per_bank = BANK // w
-            if g == 1:
-                th = spare[c % 2][:, 0 : PACK * w]
-            else:
-                th_tile = ring.tile([P, PACK * w], F32, name="th")
-                th = th_tile[:]
-            y = ring.tile([P, PACK * w], F32, name="y", bufs=4)
+            th = parts[(2 * c + g) % PACK][:, 0 : PACK * w]
+            y = ring.tile([P, PACK * w], F32, name="y", tag="staging", bufs=6)
             for t0 in range(0, PACK, per_bank):
                 e = psum.tile([P, BANK], F32, name="bank_a")
                 d = psum.tile([P, BANK], F32, name="bank_b")
@@ -294,7 +294,7 @@ def tile_list_applicant_profile_update_kernel(
         def planes(c, g, y):
             w = WIDTHS[c]
             y_bf = ring.tile([P, PACK * w], BF16, name="y_bf", bufs=3, align_bytes=64)
-            on_vector = (c, g) in ((2, 1), (3, 0), (3, 1), (4, 1))
+            on_vector = c != 1
             interleave(nc.vector.tensor_copy if on_vector else nc.scalar.copy, y_bf[:], y[:])
             at = slice(g * M + STARTS[c], g * M + STARTS[c] + w)
             nc.vector.quantize_mx(out=y_w[:, at].bitcast(FP8X4), scales=y_s[:, at], in_=y_bf[:])
@@ -303,21 +303,22 @@ def tile_list_applicant_profile_update_kernel(
                 in_=y_w[:, at].bitcast(I32),
             )
 
-        x_bf = interleave_x(0)
-        for t in (0, 1):
-            fetch_x(t, 1)
-        x_w, x_s = quantize_x(0, x_bf)
+        fetch_x_slot(3, 0)
+        x_w, x_s = quantize_x(0)
+        fetch_x_slot(3, 1)
+        lay_x_rows(2)
         for t in (2, 3):
-            fetch_x(t, 1)
+            fetch_x_slot(t, 2)
+        waiting = []
         for c in range(len(WIDTHS)):
             ys = [features(c, g, x_w, x_s) for g in range(2)]
             if c + 1 < len(WIDTHS):
-                x_w, x_s = quantize_x(c + 1, interleave_x(c + 1))
-            if c + 2 < len(WIDTHS):
-                for t in range(PACK):
-                    fetch_x(t, c + 2)
-            for g in range(2):
-                planes(c, g, ys[g])
+                x_w, x_s = quantize_x(c + 1)
+            for g, y in enumerate(waiting):
+                planes(c - 1, g, y)
+            waiting = ys
+        for g, y in enumerate(waiting):
+            planes(len(WIDTHS) - 1, g, y)
         for q in range(4):
             nc.sync.dma_start(
                 out=out_2.bitcast(I32)[:, 4 * q : 4 * q + 4, :].rearrange("g r m -> r g m"),

@@ -50,7 +50,8 @@ def tile_list_applicant_profile_update_kernel(
         tab_w = [held("tab_w%d" % a, [P, T], U32) for a in range(2)]
         tab_s = held("tab_s", [P, T], U8)
         v_w = [held("v_w%d" % a, [P, S], U32) for a in range(2)]
-        v_s = [held("v_s%d" % a, [P, S], U8) for a in range(2)]
+        v_rows = held("v_rows", [P, S], U8)
+        v_s = held("v_s", [P, 2 * S], U8)
         w2_raw = held("w2_raw", [P, 2 * 2 * PASS], U8)
         w3_raw = held("w3_raw", [P, 2 * 2 * PASS], U8)
         w2s_raw = held("w2s_raw", [P, 2 * PASS], U8)
@@ -98,30 +99,29 @@ def tile_list_applicant_profile_update_kernel(
         def shift_up(queue, dst, src):
             queue.dma_start(out=dst[0:SHIFT_ROWS, :].bitcast(I32), in_=src[4 : 4 + SHIFT_ROWS, :].bitcast(I32))
 
-        nc.vector.memset(tab_s[:].bitcast(I32), 0)
-        nc.vector.memset(v_s[1][:].bitcast(I32), 0)
+        nc.vector.memset(tab_s[32:64, :].bitcast(I32), 0)
+        nc.vector.memset(tab_s[64:128, :].bitcast(I32), 0)
+        nc.vector.memset(v_s[:].bitcast(I32), 0)
         nc.vector.memset(w3s_raw[:].bitcast(I32), 0)
         nc.vector.memset(w3_s[1][:].bitcast(I32), 0)
         nc.vector.memset(w2s_raw[:].bitcast(I32), 0)
+        nc.sync.dma_start(list1[:], offs)
+        nc.sync.dma_start(
+            out=tab_s[0:32, :].bitcast(I32), in_=tab_scales.bitcast(I32).rearrange("a b c -> b a c")
+        )
         nc.sync.dma_start(list2[:], offs2)
         load_page(0)
-        for q in range(4):
-            nc.sync.dma_start(
-                out=tab_s[32 * q : 32 * q + 8, :].bitcast(I32),
-                in_=tab_scales.bitcast(I32)[:, 4 * q : 4 * q + 4, :],
-            )
-        nc.sync.dma_start(list1[:], offs)
-        load_tab(0)
         nc.sync.dma_start(
             out=w2_raw[:].bitcast(I32).rearrange("p (a c) -> p a c", a=2),
             in_=w2_words.bitcast(I32).rearrange("a p c -> p a c"),
         )
-        load_page(1)
+        load_tab(0)
         for q in range(4):
             nc.sync.dma_start(
                 out=w2s_raw[32 * q : 32 * q + 4, :].bitcast(I32).rearrange("r (a c) -> r a c", a=2),
                 in_=w2_scales.bitcast(I32)[:, 4 * q : 4 * q + 4, :].rearrange("a r c -> r a c"),
             )
+        load_page(1)
         load_page(2)
         load_tab(1)
         w1_raw = [load_float_weight(w1[a * PASS : (a + 1) * PASS, :]) for a in range(2)]
@@ -158,14 +158,18 @@ def tile_list_applicant_profile_update_kernel(
         def fetch_x_slot(t, c):
             nc.vector.tensor_copy(x_slots(c)[:, :, t], look_up_x(t, STARTS[c], STARTS[c] + WIDTHS[c]))
 
+        nc.vector.tensor_copy(v_rows[:], tab_s[:].indirect(list1[:]))
+        for q in range(4):
+            nc.scalar.dma_start(
+                out=v_s[32 * q : 32 * q + 4, :].bitcast(I32).rearrange("r (a c) -> r a c", a=2),
+                in_=v_rows[8 * q : 8 * q + 8, :].bitcast(I32),
+            )
         fetch_old(0)
-        nc.vector.tensor_copy(v_s[0][:], tab_s[:].indirect(list1[:]))
-        shift_up(nc.scalar, v_s[1], v_s[0])
+        deal(w2_w[:].bitcast(U16), w2_raw[:].bitcast(U16))
         nc.vector.tensor_copy(v_w[0][:], tab_w[0][:].indirect(list1[:]))
+        deal(w2_s[:], w2s_raw[:])
         fetch_old(1)
         fetch_old(2)
-        deal(w2_w[:].bitcast(U16), w2_raw[:].bitcast(U16))
-        deal(w2_s[:], w2s_raw[:])
         for h in range(S // BANK):
             nc.vector.tensor_copy(
                 v_w[1][:, h * BANK : (h + 1) * BANK],
@@ -183,7 +187,7 @@ def tile_list_applicant_profile_update_kernel(
                         lhsT=w2_w[:, 2 * P * at : 2 * P * (at + 1)].bitcast(FP4X4),
                         lhsT_scale=w2_s[:, P * at : P * (at + 1)],
                         rhs=v_w[a][:, cols].bitcast(FP8X4),
-                        rhs_scale=v_s[a][:, cols],
+                        rhs_scale=v_s[:, a * S + h * BANK : a * S + (h + 1) * BANK],
                         start=(a == 0),
                         stop=(a == 1),
                     )
@@ -201,7 +205,7 @@ def tile_list_applicant_profile_update_kernel(
                         lhsT=w1_w[a][:, P * t : P * (t + 1)].bitcast(FP8X4),
                         lhsT_scale=w1_s[a][:, P * t : P * (t + 1)],
                         rhs=v_w[a][:, cols].bitcast(FP8X4),
-                        rhs_scale=v_s[a][:, cols],
+                        rhs_scale=v_s[:, a * S + h * BANK : a * S + (h + 1) * BANK],
                         start=(a == 0),
                         stop=(a == 1),
                     )

from contextlib import ExitStack

import concourse.mybir as mybir

K, H, N, T, S, T2, M = 1024, 512, 1024, 4096, 1024, 2048, 1024
FLOPS = 2 * (2 * K * H * S) + 2 * (2 * H * N * M)

F32 = mybir.dt.float32
BF16 = mybir.dt.bfloat16
I32 = mybir.dt.int32
U32 = mybir.dt.uint32
U16 = mybir.dt.uint16
U8 = mybir.dt.uint8
FP8X4 = mybir.dt.float8_e4m3fn_x4
FP4X4 = mybir.dt.float4_e2m1fn_x4
ALU = mybir.AluOpType
ACT = mybir.ActivationFunctionType

P = 128
PACK = 4
PASS = P * PACK
BANK = 512
WIDTHS = (256, 512, 256)
STARTS = [sum(WIDTHS[:c]) for c in range(len(WIDTHS))]
SHIFT_ROWS = 112
PER_COL = 16


def interleave(copy, dst, src):
    copy(dst.rearrange("p (c i t) -> p c t i", i=4, t=PACK), src.rearrange("p (t c i) -> p c t i", i=4, t=PACK))


def tile_list_applicant_profile_update_kernel(
    tc, tab_words, tab_scales, offs, offs2, offs3, page0, w1, w2_words, w2_scales, w3_words, w3_scales, w4, gain,
    out_0, out_1, out_2,
):
    nc = tc.nc
    with ExitStack() as ctx:
        keep = ctx.enter_context(tc.tile_pool(name="keep", bufs=1))
        ring = ctx.enter_context(tc.tile_pool(name="ring", bufs=2))
        psum = ctx.enter_context(tc.psum_pool(name="psum", bufs=4))

        def held(name, shape, dtype):
            return keep.tile(shape, dtype, name=name, align_bytes=64)

        list1 = held("list1", [P, S // PER_COL], U16)
        list2 = held("list2", [P, S // PER_COL], U16)
        list3 = held("list3", [P, M // PER_COL], U16)
        page = [held("page%d" % t, [P, T2], F32) for t in range(PACK)]
        tab_w = [held("tab_w%d" % a, [P, T], U32) for a in range(2)]
        tab_s = held("tab_s", [P, T], U8)
        v_w = [held("v_w%d" % a, [P, S], U32) for a in range(2)]
        v_rows = held("v_rows", [P, S], U8)
        v_s = held("v_s", [P, 2 * S], U8)
        w2_raw = held("w2_raw", [P, 2 * 2 * PASS], U8)
        w3_raw = held("w3_raw", [P, 2 * 2 * PASS], U8)
        w2s_raw = held("w2s_raw", [P, 2 * PASS], U8)
        w3s_raw = held("w3s_raw", [P, PASS], U8)
        w2_w = held("w2_w", [P, 2 * 2 * PASS], U8)
        w3_w = held("w3_w", [P, 2 * 2 * PASS], U8)
        w2_s = held("w2_s", [P, 2 * PASS], U8)
        w3_s = [held("w3_s%d" % g, [P, PASS], U8) for g in range(2)]
        w1_w = [held("w1_w%d" % a, [P, PASS], U32) for a in range(2)]
        w1_s = [held("w1_s%d" % a, [P, PASS], U8) for a in range(2)]
        w4_w = [held("w4_w%d" % g, [P, PASS], U32) for g in range(2)]
        w4_s = [held("w4_s%d" % g, [P, PASS], U8) for g in range(2)]
        gains = held("gains", [P, 2, PACK], F32)
        parts = [held("parts%d" % t, [P, 2 * S], F32) for t in range(PACK)]
        y_w = held("y_w", [P, 2 * M], U32)
        y_s = held("y_s", [P, 2 * M], U8)

        page_rows = page0.rearrange("(p t) c -> t p c", t=PACK)

        def load_page(t):
            nc.sync.dma_start(out=page[t][:], in_=page_rows[t])

        def load_tab(a):
            nc.sync.dma_start(out=tab_w[a][:].bitcast(I32), in_=tab_words[a].rearrange("p c i -> p (c i)").bitcast(I32))

        def load_float_weight(rows):
            raw = ring.tile([P, PACK, PASS], F32, name="w_raw", tag="staging", bufs=6)
            nc.sync.dma_start(out=raw[:], in_=rows.rearrange("(p j) c -> p j c", j=PACK))
            return raw

        def quantize_weight(raw, words, scales):
            dealt = ring.tile([P, PACK * PASS], BF16, name="w_dealt", align_bytes=64)
            nc.scalar.copy(
                dealt[:].rearrange("p (t m j) -> p m t j", t=PACK, j=PACK),
                raw[:].rearrange("p j (m t) -> p m t j", t=PACK),
            )
            nc.vector.quantize_mx(out=words[:].bitcast(FP8X4), scales=scales[:], in_=dealt[:])

        def deal(dst, src):
            nc.vector.tensor_copy(
                dst.rearrange("p (a t m) -> p a m t", t=PACK, m=P),
                src.rearrange("p (a m t) -> p a m t", t=PACK, m=P),
            )

        def shift_up(queue, dst, src):
            queue.dma_start(out=dst[0:SHIFT_ROWS, :].bitcast(I32), in_=src[4 : 4 + SHIFT_ROWS, :].bitcast(I32))

        nc.vector.memset(tab_s[32:64, :].bitcast(I32), 0)
        nc.vector.memset(tab_s[64:128, :].bitcast(I32), 0)
        nc.vector.memset(v_s[:].bitcast(I32), 0)
        nc.vector.memset(w3s_raw[:].bitcast(I32), 0)
        nc.vector.memset(w3_s[1][:].bitcast(I32), 0)
        nc.vector.memset(w2s_raw[:].bitcast(I32), 0)
        nc.sync.dma_start(list1[:], offs)
        nc.sync.dma_start(
            out=tab_s[0:32, :].bitcast(I32), in_=tab_scales.bitcast(I32).rearrange("a b c -> b a c")
        )
        nc.sync.dma_start(list2[:], offs2)
        load_page(0)
        nc.sync.dma_start(
            out=w2_raw[:].bitcast(I32).rearrange("p (a c) -> p a c", a=2),
            in_=w2_words.bitcast(I32).rearrange("a p c -> p a c"),
        )
        load_tab(0)
        for q in range(4):
            nc.sync.dma_start(
                out=w2s_raw[32 * q : 32 * q + 4, :].bitcast(I32).rearrange("r (a c) -> r a c", a=2),
                in_=w2_scales.bitcast(I32)[:, 4 * q : 4 * q + 4, :].rearrange("a r c -> r a c"),
            )
        load_page(1)
        load_page(2)
        load_tab(1)
        w1_raw = [load_float_weight(w1[a * PASS : (a + 1) * PASS, :]) for a in range(2)]
        load_page(3)
        nc.sync.dma_start(list3[:], offs3)
        w4_raw = [load_float_weight(w4[:, g * PASS : (g + 1) * PASS]) for g in range(2)]
        nc.sync.dma_start(out=w3_raw[:].bitcast(I32), in_=w3_words.bitcast(I32)[0])
        for q in range(4):
            nc.sync.dma_start(
                out=w3s_raw[32 * q : 32 * q + 8, :].bitcast(I32),
                in_=w3_scales.bitcast(I32)[0, 4 * q : 4 * q + 4, :].rearrange("r (g c) -> g r c", g=2),
            )
        nc.sync.dma_start(out=gains[:], in_=gain.rearrange("(g p t) -> p g t", g=2, t=PACK))

        def fetch_old(t):
            nc.vector.tensor_copy(parts[t][:, 0:S], page[t][:].indirect(list2[:]))

        x_rows = held("x_rows", [P, 2 * M], BF16)
        x_bf = [held("x_bf%d" % i, [P, PACK * WIDTHS[i]], BF16) for i in range(2)]

        def x_slots(c):
            return x_bf[c % 2][:].rearrange("p (m t) -> p m t", t=PACK)

        def look_up_x(t, start, stop):
            return page[t][:].indirect(list3[:, start // PER_COL : stop // PER_COL])

        def fetch_x_row(t):
            nc.vector.tensor_copy(x_rows[:, t * M : (t + 1) * M], look_up_x(t, 0, M))

        def lay_x_rows(c):
            rows = x_rows[:].rearrange("p (t m) -> p m t", t=2)
            nc.scalar.copy(x_slots(c)[:, :, 0:2], rows[:, STARTS[c] : STARTS[c] + WIDTHS[c], :])

        def fetch_x_slot(t, c):
            nc.vector.tensor_copy(x_slots(c)[:, :, t], look_up_x(t, STARTS[c], STARTS[c] + WIDTHS[c]))

        nc.vector.tensor_copy(v_rows[:], tab_s[:].indirect(list1[:]))
        for q in range(4):
            nc.scalar.dma_start(
                out=v_s[32 * q : 32 * q + 4, :].bitcast(I32).rearrange("r (a c) -> r a c", a=2),
                in_=v_rows[8 * q : 8 * q + 8, :].bitcast(I32),
            )
        fetch_old(0)
        deal(w2_w[:].bitcast(U16), w2_raw[:].bitcast(U16))
        nc.vector.tensor_copy(v_w[0][:], tab_w[0][:].indirect(list1[:]))
        deal(w2_s[:], w2s_raw[:])
        fetch_old(1)
        fetch_old(2)
        for h in range(S // BANK):
            nc.vector.tensor_copy(
                v_w[1][:, h * BANK : (h + 1) * BANK],
                tab_w[1][:].indirect(list1[:, h * BANK // PER_COL : (h + 1) * BANK // PER_COL]),
            )

        def larger(t):
            for h in range(S // BANK):
                cols = slice(h * BANK, (h + 1) * BANK)
                base = psum.tile([P, BANK], F32, name="bank_a")
                for a in range(2):
                    at = a * PACK + t
                    nc.tensor.matmul_mx(
                        out=base[:],
                        lhsT=w2_w[:, 2 * P * at : 2 * P * (at + 1)].bitcast(FP4X4),
                        lhsT_scale=w2_s[:, P * at : P * (at + 1)],
                        rhs=v_w[a][:, cols].bitcast(FP8X4),
                        rhs_scale=v_s[:, a * S + h * BANK : a * S + (h + 1) * BANK],
                        start=(a == 0),
                        stop=(a == 1),
                    )
                nc.vector.tensor_tensor(
                    parts[t][:, S + h * BANK : S + (h + 1) * BANK], parts[t][:, cols], base[:], ALU.max
                )

        def smaller(t):
            for h in range(S // BANK):
                cols = slice(h * BANK, (h + 1) * BANK)
                cap = psum.tile([P, BANK], F32, name="bank_b")
                for a in range(2):
                    nc.tensor.matmul_mx(
                        out=cap[:],
                        lhsT=w1_w[a][:, P * t : P * (t + 1)].bitcast(FP8X4),
                        lhsT_scale=w1_s[a][:, P * t : P * (t + 1)],
                        rhs=v_w[a][:, cols].bitcast(FP8X4),
                        rhs_scale=v_s[:, a * S + h * BANK : a * S + (h + 1) * BANK],
                        start=(a == 0),
                        stop=(a == 1),
                    )
                nc.vector.tensor_tensor(parts[t][:, cols], parts[t][:, cols], cap[:], ALU.min)

        def put(t):
            nc.vector.tensor_tensor(page[t][:].indirect(list2[:]), parts[t][:, 0:S], parts[t][:, S : 2 * S], ALU.add)

        for t in range(PACK - 1):
            larger(t)
        quantize_weight(w1_raw[0], w1_w[0], w1_s[0])
        fetch_old(PACK - 1)
        quantize_weight(w1_raw[1], w1_w[1], w1_s[1])
        larger(PACK - 1)
        smaller(0)
        for t in range(PACK):
            if t + 1 < PACK:
                smaller(t + 1)
            if t in (1, 2):
                fetch_x_row(t - 1)
            if t == 2:
                for c in (0, 1):
                    lay_x_rows(c)
            if t == 3:
                for c in (0, 1):
                    fetch_x_slot(2, c)
            put(t)
            if t == 0:
                for g in range(2):
                    quantize_weight(w4_raw[g], w4_w[g], w4_s[g])
                deal(w3_w[:].bitcast(U16), w3_raw[:].bitcast(U16))
                deal(w3_s[0][:], w3s_raw[:])
                shift_up(nc.sync, w3_s[1], w3_s[0])

        def quantize_x(c):
            w = WIDTHS[c]
            x_w = ring.tile([P, w], U32, name="x_w", align_bytes=64)
            x_s = ring.tile([P, w], U8, name="x_s", align_bytes=64)
            nc.vector.quantize_mx(out=x_w[:].bitcast(FP8X4), scales=x_s[:], in_=x_bf[c % 2][:])
            return x_w, x_s

        def features(c, g, x_w, x_s):
            w = WIDTHS[c]
            per_bank = BANK // w
            th = parts[(2 * c + g) % PACK][:, 0 : PACK * w]
            y = ring.tile([P, PACK * w], F32, name="y", tag="staging", bufs=6)
            for t0 in range(0, PACK, per_bank):
                e = psum.tile([P, BANK], F32, name="bank_a")
                d = psum.tile([P, BANK], F32, name="bank_b")
                for i in range(per_bank):
                    t = t0 + i
                    gt = g * PACK + t
                    nc.tensor.matmul_mx(
                        out=e[:, i * w : (i + 1) * w],
                        lhsT=w3_w[:, 2 * P * gt : 2 * P * (gt + 1)].bitcast(FP4X4),
                        lhsT_scale=w3_s[g][:, P * t : P * (t + 1)],
                        rhs=x_w[:].bitcast(FP8X4),
                        rhs_scale=x_s[:],
                        start=True,
                        stop=True,
                    )
                for i in range(per_bank):
                    t = t0 + i
                    nc.tensor.matmul_mx(
                        out=d[:, i * w : (i + 1) * w],
                        lhsT=w4_w[g][:, P * t : P * (t + 1)].bitcast(FP8X4),
                        lhsT_scale=w4_s[g][:, P * t : P * (t + 1)],
                        rhs=x_w[:].bitcast(FP8X4),
                        rhs_scale=x_s[:],
                        start=True,
                        stop=True,
                    )
                nc.scalar.activation(th[:, t0 * w : t0 * w + BANK], e[:], ACT.Tanh)
                for i in range(per_bank):
                    t = t0 + i
                    nc.vector.scalar_tensor_tensor(
                        y[:, t * w : (t + 1) * w],
                        th[:, t * w : (t + 1) * w],
                        gains[:, g, t : t + 1],
                        d[:, i * w : (i + 1) * w],
                        ALU.mult,
                        ALU.add,
                    )
            nc.sync.dma_start(
                out=out_0[g * PASS : (g + 1) * PASS, STARTS[c] : STARTS[c] + w].rearrange("(p t) m -> p t m", t=PACK),
                in_=y[:].rearrange("p (t m) -> p t m", t=PACK),
            )
            return y

        def planes(c, g, y):
            w = WIDTHS[c]
            y_bf = ring.tile([P, PACK * w], BF16, name="y_bf", bufs=3, align_bytes=64)
            on_vector = c != 1
            interleave(nc.vector.tensor_copy if on_vector else nc.scalar.copy, y_bf[:], y[:])
            at = slice(g * M + STARTS[c], g * M + STARTS[c] + w)
            nc.vector.quantize_mx(out=y_w[:, at].bitcast(FP8X4), scales=y_s[:, at], in_=y_bf[:])
            nc.sync.dma_start(
                out=out_1[g].rearrange("p m t -> p (m t)").bitcast(I32)[:, STARTS[c] : STARTS[c] + w],
                in_=y_w[:, at].bitcast(I32),
            )

        fetch_x_slot(3, 0)
        x_w, x_s = quantize_x(0)
        fetch_x_slot(3, 1)
        lay_x_rows(2)
        for t in (2, 3):
            fetch_x_slot(t, 2)
        waiting = []
        for c in range(len(WIDTHS)):
            ys = [features(c, g, x_w, x_s) for g in range(2)]
            if c + 1 < len(WIDTHS):
                x_w, x_s = quantize_x(c + 1)
            for g, y in enumerate(waiting):
                planes(c - 1, g, y)
            waiting = ys
        for g, y in enumerate(waiting):
            planes(len(WIDTHS) - 1, g, y)
        for q in range(4):
            nc.sync.dma_start(
                out=out_2.bitcast(I32)[:, 4 * q : 4 * q + 4, :].rearrange("g r m -> r g m"),
                in_=y_s[32 * q : 32 * q + 4, :].bitcast(I32).rearrange("r (g m) -> r g m", g=2),
            )
